import numpy as np, ml_dtypes
CORES = [2,3,42,43,82,83,122,123]
N = 8
BF = ml_dtypes.bfloat16
def gentries(a):
    return np.ascontiguousarray(a.reshape(8, 16, -1).transpose(0, 2, 1)).reshape(8, -1)
def gtable(e):
    e = np.asarray(e); return np.ascontiguousarray(e.reshape(8, -1, 16).transpose(0, 2, 1)).reshape(128, -1).astype(np.int32)
S, V, RO, C = 1, 4096, 3, 20
def pairs(rng, F):
    o = np.argsort(rng.random((N, 8, RO, S, V)), axis=-1)
    w = np.ascontiguousarray(o.reshape(N, 8, RO, S, V // 2, 2)[..., ::-1]).reshape(N, 8, RO, S, V)
    w[..., :F] = o[..., :F]
    m = np.empty_like(o); np.put_along_axis(m, o, w, -1)
    return m
def whole_in(rng, size):
    return np.rint(size * (2.0 * rng.random((N, 8, 16, S, V)) - 1.0)).astype(np.int64)
def parts(rng):
    x = whole_in(rng, rng.choice(np.array([3.0, 10.0, 30.0, 60.0]), (N, 8, 1, S, V)))
    p = np.argsort(rng.random((N, 8, S, V)), axis=-1)
    return x, p, pairs(rng, 2 * (V // 64))
def pack(x, p, m):
    return {"x": np.ascontiguousarray(x.reshape(N, 128, S * V)).astype(np.float32).astype(BF),
            "p": np.stack([gtable(a.reshape(8, -1)) for a in p]), "mate": np.stack([gtable(a.reshape(8, -1)) for a in m])}
def put(x, p, m, g, xs, ps, ms):
    x[:, g] = xs.reshape(N, S, 16, V).transpose(0, 2, 1, 3)
    p[:, g] = ps.reshape(N, S, V)
    m[:, g, :len(ms)] = np.reshape(ms, (-1, N, S, V)).transpose(1, 0, 2, 3)
def sides(rng):
    Z = N * S; h = V // 2
    o = np.argsort(rng.random((Z, V)), axis=-1)
    b = np.empty((Z, V), np.int64); ps = np.empty((Z, V), np.int64); ms = np.empty((Z, V), np.int64)
    np.put_along_axis(b, o, np.tile(np.where(np.arange(V) < h, 1, -1), (Z, 1)), 1)
    np.put_along_axis(ps, o, np.roll(o, -1, axis=0), 1)
    a = o[:, :h]; c = np.take_along_axis(o[:, h:], np.argsort(rng.random((Z, h)), axis=-1), 1)
    np.put_along_axis(ms, a, c, 1); np.put_along_axis(ms, c, a, 1)
    return b, ps, ms
def link(x, p, back, used, mt, z, a, e):
    b = back[z, e]; u = (z + 1) % (N * S)
    if used[z, a] or used[z, b]: return False
    if a != b:
        i = p[z, a]
        va, vb, vi, ve = x[z, :, a], x[z, :, b], x[u, :, i], x[u, :, e]
        if np.sum(np.abs(va - vi) + np.abs(vb - ve) - np.abs(va - ve) - np.abs(vb - vi)) <= 0: return False
        mt[z, a] = b; mt[z, b] = a
    used[z, a] = True; used[z, b] = True
    return True
def grow(rng):
    Z = N * S; h = C // 2
    x = rng.integers(-60, 61, (Z, 16, V))
    x[:, :4] = np.where(rng.random((Z, 1, V)) < 0.0625, 60 - h, 60) * np.array([1, 1, -1, 1])[None, :, None]
    p = np.argsort(rng.random((Z, V)), axis=-1); m = np.tile(np.arange(V), (RO, Z, 1)); x0 = x; p0 = p
    for t in range(RO):
        if t > 0:
            back = np.argsort(p, axis=-1); used = np.zeros((Z, V), bool); w = x[:, 0]; hi = 60 + t * h; want = 32 >> (t - 1)
            hot = [np.flatnonzero(w[z] == hi) for z in range(Z)]
            for z in range(Z):
                l = (z - 1) % Z; u = (z + 1) % Z
                for c in rng.permutation(np.flatnonzero(w[z] == hi - h))[:want]:
                    if any(link(x, p, back, used, m[t], l, e, c) for e in rng.permutation(hot[l])[:16]):
                        any(link(x, p, back, used, m[t], z, c, e) for e in rng.permutation(hot[u])[:16])
                if t < RO - 1:
                    for c in rng.permutation(np.flatnonzero((w[z] == 60) & (w[u][p[z]] >= 60) & ~used[z]))[:want]:
                        if not used[z, c] and any(link(x, p, back, used, m[t], l, e, c) for e in rng.permutation(hot[l])[:16]): used[z, c] = True
        p = np.take_along_axis(p, m[t], 1)
        succ = np.take_along_axis(np.roll(x, -1, axis=0), p[:, None, :], 2)
        pred = np.roll(np.take_along_axis(x, np.argsort(p, axis=-1)[:, None, :], 2), 1, axis=0)
        x = x + np.clip(pred + succ - 2 * x, -C, C)
    return x0, p0, m
def setup_inputs(rng):
    return pack(*parts(rng))
def setup_inputs_near(rng):
    x, p, m = parts(rng); x = whole_in(rng, 60.0)
    m[:, :, 0] = pairs(rng, 0)[:, :, 0]; m0 = m[:, :, 0]; ar = np.arange(V)
    x = np.take_along_axis(x, np.minimum(ar, m0)[:, :, None], 4)
    co = np.arange(16)[None, None, :, None, None]; late = (ar > m0)[:, :, None]
    for i in range(2):
        x = x + (rng.integers(0, 16, (N, 8, 1, S, V)) == co) * rng.integers(-3, 4, (N, 8, 1, S, V)) * late
    return pack(np.clip(x, -60, 60), p, m)
def setup_inputs_ties(rng):
    x, p, m = parts(rng)
    x = rng.integers(-1, 2, (N, 8, 16, S, V)) * (np.arange(16)[None, :] <= np.arange(8)[:, None])[None, :, :, None, None]
    return pack(x, p, m)
def setup_inputs_still(rng):
    x, p, m = parts(rng); i = np.arange(V)
    p[:, 0] = i; p[:, 1] = V - 1 - i; p[:, 2] = np.roll(i, 1); p[:, 7] = np.roll(i, -1)
    m[:, 0] = i; m[:, 1] = i ^ 1; m[:, 2] = V - 1 - i; m[:, 4] = m[:, 4, :1].copy(); m[:, 5, RO - 1] = i
    x[:, 3] = x[:1, 3, :, :1, :1].copy()
    return pack(x, p, m)
def setup_inputs_ends(rng):
    x, p, m = parts(rng)
    v = rng.choice(np.array([60, 60, 59, 50, 45]), (N, 8, 16, S, V)); x = np.where(rng.random((N, 8, 16, S, V)) < 0.5, v, -v)
    x[:, 0] = v[:, 0]
    x[:, 1] = 60 * (1 - 2 * (np.arange(N * S).reshape(N, 1, S, 1) & 1))
    x[:, 2] = v[:, 2] * (1 - 2 * rng.integers(0, 2, (N, 1, S, V)))
    Z = N * S; turn = (1 - 2 * (np.arange(Z) & 1))[:, None, None]; odd = (np.arange(Z) & 1)[:, None] == 1
    b, ps, ms = sides(rng)
    put(x, p, m, 3, b[:, None, :] * turn * rng.integers(50, 61, (Z, 16, V)), ps, ms[None])
    b, ps, ms = sides(rng)
    put(x, p, m, 4, b[:, None, :] * np.where(np.arange(16)[None, :, None] < 8, turn, 1) * rng.integers(57, 61, (Z, 16, V)), ps, ms[None])
    put(x, p, m, 5, *grow(rng))
    b, ps, ms = sides(rng); dip = (b > 0) == odd
    xs = rng.integers(-2, 3, (Z, 16, V))
    xs[:, :2] = b[:, None, :] * np.where(dip[:, None, :], 60 - C // 2 + rng.integers(0, 3, (Z, 2, V)), 60)
    xs[:, 2:4] = b[:, None, :] * turn * 60
    xs[:, 4] = rng.integers(-6, 7, (Z, V))
    put(x, p, m, 6, xs, ps, np.stack([np.tile(np.arange(V), (Z, 1)), ms]))
    return pack(x, p, m)
def setup_inputs_spread(rng):
    x, p, m = parts(rng)
    x = whole_in(rng, 60.0 * np.exp2(-rng.integers(0, 7, (N, 8, 1, S, V)).astype(np.float64)) * (rng.random((N, 8, 1, S, V)) > 0.0625))
    return pack(x, p, m)
def check_inputs(d):
    bad = []; i = np.arange(V)
    a = np.asarray(d["x"]).astype(np.float64)
    if not (np.all(np.abs(a) <= 60) and np.all(a == np.rint(a))): bad.append("x whole from -60 to 60")
    q = np.stack([gentries(b) for b in d["p"]]).reshape(N, 8, S, V)
    if not np.all(np.sort(q, axis=-1) == i): bad.append("p permutations")
    m = np.stack([gentries(b) for b in d["mate"]]).reshape(N, 8, RO, S, V).astype(np.int64)
    if np.min(m) < 0 or np.max(m) > V - 1: bad.append("range of mate")
    elif not np.all(np.take_along_axis(m, m, -1) == i): bad.append("mate of the mate")
    return bad
def reference(x, p, mate):
    Z = N * S
    X = x.astype(np.float32).astype(np.int32).reshape(N, 8, 16, S, V).transpose(0, 3, 1, 2, 4).reshape(Z, 8, 16, V)
    P = np.stack([gentries(a) for a in p]).astype(np.int64).reshape(N, 8, S, V).transpose(0, 2, 1, 3).reshape(Z, 8, V)
    M = np.stack([gentries(a) for a in mate]).astype(np.int64).reshape(N, 8, RO, S, V).transpose(2, 0, 3, 1, 4).reshape(RO, Z, 8, V)
    for rnd in range(RO):
        m = M[rnd]
        s = np.take_along_axis(np.roll(X, -1, axis=0), P[:, :, None, :], 3)
        t = np.take_along_axis(s, m[:, :, None, :], 3)
        D = np.add.reduce(np.abs(X - s), axis=2) - np.add.reduce(np.abs(X - t), axis=2)
        go = D + np.take_along_axis(D, m, 2) > 0
        P = np.where(go, np.take_along_axis(P, m, 2), P)
        succ = np.where(go[:, :, None, :], t, s)
        back = np.argsort(P, axis=-1)
        pred = np.roll(np.take_along_axis(X, back[:, :, None, :], 3), 1, axis=0)
        X = X + np.clip(pred + succ - 2 * X, -C, C)
    yx = X.reshape(N, S, 8, 16, V).transpose(0, 2, 3, 1, 4).reshape(N, 128, S * V)
    yp = P.reshape(N, S, 8, V).transpose(0, 2, 1, 3).reshape(N, 8, S * V)
    return {"yx": yx.astype(np.float32).astype(BF), "yp": np.stack([gtable(a) for a in yp]).astype(np.float32)}

@@ -1,0 +1,478 @@
+from concourse.bass import DstId, RemoteDMATransfer
+from concourse.mybir import AluOpType as Op, ActivationFunctionType as Fn
+
+V_, RO, CL = 4096, 3, 20.0
+U = 512
+BL = 2 * U
+K = V_ // 16
+H = K // 2
+HANDED = (0, 1, 2)
+
+SCRATCH = {"ps": ("psum", [128, 4096], "float32")}
+for _t in range(RO + 1):
+    SCRATCH["X%d" % _t] = ("sbuf", [128, V_], "bfloat16")
+    SCRATCH["B%d" % _t] = ("sbuf", [128, K], "uint16")
+for _t in range(RO):
+    SCRATCH["Y%d" % _t] = ("sbuf", [128, V_], "bfloat16")
+    SCRATCH["Z%d" % _t] = ("sbuf", [128, V_], "bfloat16")
+    SCRATCH["Bin%d" % _t] = ("sbuf", [128, K], "uint16")
+for _n in ("M1", "M2", "S", "R1", "Dif", "GD", "tab", "W1", "W", "Cl", "Xm2"):
+    SCRATCH[_n] = ("sbuf", [128, V_], "bfloat16")
+SCRATCH.update({
+    "pin": ("sbuf", [128, K], "int32"), "min": ("sbuf", [128, RO * K], "int32"),
+    "m16": ("sbuf", [128, RO * K], "uint16"), "P16": ("sbuf", [128, K], "uint16"), "Pm16": ("sbuf", [128, K], "uint16"),
+    "Pd": ("sbuf", [128, K], "float32"), "dP": ("sbuf", [128, K], "float32"), "dT": ("sbuf", [128, K], "float32"),
+    "Pc": ("sbuf", [128, K], "float16"), "Tc": ("sbuf", [128, K], "float16"), "ypf": ("sbuf", [128, K], "float32"),
+    "vf": ("sbuf", [128, K], "float32"), "vc": ("sbuf", [128, K], "float32"), "c16": ("sbuf", [128, K], "float32"),
+    "rr": ("sbuf", [128, K], "bfloat16"),
+    "pi": ("sbuf", [128, 1], "int32"), "ki": ("sbuf", [128, 1], "int32"), "gi": ("sbuf", [128, 1], "int32"),
+    "kf": ("sbuf", [128, 1], "float32"), "gf": ("sbuf", [128, 1], "float32"), "bT": ("sbuf", [128, 1], "float32"),
+    "qr": ("sbuf", [128, 16], "float32"), "A16": ("sbuf", [128, 16], "float32"), "C16": ("sbuf", [128, 16], "float32"),
+    "gr": ("sbuf", [128, 128], "float32"), "dg": ("sbuf", [128, 128], "float32"),
+    "BD": ("sbuf", [128, 128], "bfloat16"), "I1": ("sbuf", [128, 128], "bfloat16"),
+    "In": ("sbuf", [128, 128], "bfloat16"), "I2": ("sbuf", [128, 128], "bfloat16"),
+    "Zp": ("sbuf", [128, 144], "bfloat16"), "Zn": ("sbuf", [128, 144], "bfloat16"),
+    "Xs": ("sbuf", [128, 2048], "bfloat16"),
+})
+SEMAPHORES = (["sV", "sA", "sT", "sG", "ldp", "ldm", "ldn", "sent", "out"] + ["ldx%d" % q for q in range(4)]
+              + ["arr%s%d" % (n, t) for n in "YZB" for t in range(RO)])
+
+
+def popcount(m):
+    return bin(m).count("1")
+
+
+def ring(T, topo):
+    n, taken, out = len(T.cores), [], {}
+    for r, c in enumerate(T.cores):
+        prv, nxt = T.cores[(r - 1) % n], T.cores[(r + 1) % n]
+        far = prv if topo.chip(prv) != topo.chip(c) else nxt
+        h = [x for x in topo.cores_of(c) if T.rank_of(x) is None and x not in taken
+             and topo.die(x) != topo.die(c) and topo.may_write(x, far)][0]
+        taken.append(h)
+        out[c] = {"prv": prv, "nxt": nxt, "far": far, "help": h, "rest": topo.mask(c, h) & ~topo.mask(c, far)}
+    return out
+
+
+def helper_program(g, core, R, T, topo):
+    far, got = R["far"], popcount(R["rest"])
+    a, m, sent = topo.addr(far), topo.mask(core, far), 0
+    for t in range(RO):
+        if far == R["prv"]:
+            pieces = [("arr%s%d" % (s, t), T["Y%d" % t][:, q * BL:q * BL + U], "arrY%d" % t)
+                      for s, q in zip("YZB", HANDED)]
+        else:
+            pieces = [("arrZ%d" % t, T["Z%d" % t][:, 0:2 * BL], "arrZ%d" % t)]
+        for here, ap, there in pieces:
+            g.wait_ge(T.sem[here], got)
+            g.remote_dma(ap, ap, T.sem[there], T.sem.sent, a[1], a[0], m)
+            sent += popcount(m)
+    g.wait_ge(T.sem.sent, sent)
+
+
+def rank_program(g, core, T, topo):
+    RG = ring(T, topo)
+    if T.rank_of(core) is None:
+        for c in T.cores:
+            if RG[c]["help"] == core:
+                helper_program(g, core, RG[c], T, topo)
+        return
+    R = RG[core]
+    prv, nxt, hlp = R["prv"], R["nxt"], R["help"]
+    prv_far = R["far"] == prv
+    Q = {"V": g.vector, "A": g.scalar, "T": g.tensor, "G": g, "S": g.sync}
+    ps = T.ps
+
+    cnt = {e: 0 for e in Q}
+    clock = {e: {} for e in Q}
+    snap = {}
+    writer, readers = {}, {}
+
+    def need(e, ev):
+        s, v = ev
+        if e == "T" and s == "sT":
+            return
+        if clock[e].get(s, 0) >= v:
+            return
+        Q[e].wait_ge(T.sem[s], v)
+        for a, b in snap.get(ev, {s: v}).items():
+            if clock[e].get(a, 0) < b:
+                clock[e][a] = b
+
+    def before(e, r, w):
+        evs = [writer[k] for k in r if k in writer]
+        for k in w:
+            if k in writer:
+                evs.append(writer[k])
+            evs += readers.get(k, [])
+        best = {}
+        for s, v in evs:
+            best[s] = max(best.get(s, 0), v)
+        for s in sorted(best):
+            need(e, (s, best[s]))
+
+    def op(e, r, w, f):
+        before(e, r, w)
+        ins = f()
+        cnt[e] += 1
+        ev = ("s" + e, cnt[e])
+        ins.then_inc(T.sem["s" + e], 1)
+        c = dict(clock[e])
+        c[ev[0]] = ev[1]
+        snap[ev] = c
+        for k in r:
+            readers.setdefault(k, []).append(ev)
+        for k in w:
+            writer[k] = ev
+            readers[k] = []
+
+    def un(name, u, n=1):
+        return T[name][:, u * U:(u + n) * U]
+
+    def ks(name, u=0, n=8):
+        return ["%s.%d" % (name, x) for x in range(u, u + n)]
+
+    def lst(name, u, n, o=0):
+        return T[name][:, o + 32 * u:o + 32 * (u + n)]
+
+    def bank(b, n=1):
+        return ps[:, b * U:(b + n) * U]
+
+    def bk(b, n=1):
+        return ["b%d" % x for x in range(b, b + n)]
+
+    def seam(b):
+        return ps[:, (b + 1) * U - H:(b + 1) * U + H]
+
+    TAB = ks("tab")
+    PE = seam(6)
+    V, A, PE_ = g.vector, g.scalar, g.tensor
+
+    def mm(terms, u, b, start=True, stop=True, n=1):
+        for x in range(n):
+            def f():
+                for j, (mat, name) in enumerate(terms):
+                    ins = PE_.matmul(bank(b + x), T[mat][:], un(name, u + x),
+                                     start and j == 0, stop and j == len(terms) - 1)
+                return ins
+            op("T", [m for m, _ in terms] + ["%s.%d" % (nm, u + x) for _, nm in terms], bk(b + x), f)
+
+    def fold(name, q, z, start, stop, n=1, b=6):
+        e0 = (b + 1) * U - H
+
+        def f():
+            for i in range(16):
+                ins = PE_.matmul(ps[:, e0 + 64 * q:e0 + 64 * (q + n)], T[z][:, 15 - i:143 - i],
+                                 T[name][:, q * BL + i:(q + n) * BL:16], start and i == 0, stop and i == 15)
+            return ins
+        op("T", [z] + ks(name, 2 * q, 2 * n), bk(b + q // 2), f)
+
+    def table(src, engs, keys):
+        for j in range(8):
+            b = j % 4
+
+            def f():
+                for h in (0, 1):
+                    i = j + 8 * h
+                    ins = PE_.matmul(ps[:, b * U + h:(b + 1) * U:2], T.Xs[:, 128 * i:128 * (i + 1)], T[src][:],
+                                     True, True)
+                return ins
+            op("T", keys + ["Xs.%d" % j, "Xs.%d" % (j + 8)], bk(b), f)
+            o = T.tab[:, j::8]
+            if engs[j] == "V":
+                op("V", ["bT"], [TAB[j]] + bk(b), lambda: V.tensor_scalar(o, bank(b), T.bT[:], 0.0, Op.add, Op.max))
+            else:
+                op("A", ["bT"], [TAB[j]] + bk(b), lambda: A.activation(o, bank(b), Fn.Relu, bias=T.bT[:]))
+
+    def pick(lname, o, engs, lk):
+        for q in range(4):
+            w = T.tab[:, 0:V_].indirect(lst(lname, 2 * q, 2, o))
+            out = un("GD", 2 * q, 2)
+            if engs[q] == "V":
+                op("V", TAB + [lk], ks("GD", 2 * q, 2),
+                   lambda: V.tensor_scalar(out, w, 256.0, 256.0, Op.min, Op.subtract))
+            else:
+                op("A", TAB + [lk], ks("GD", 2 * q, 2), lambda: A.activation(out, w, Fn.Relu, bias=256.0, scale=-1.0))
+            fold("GD", q, "Zp" if engs[q] == "V" else "Zn", True, True)
+
+    def mates_links():
+        op("V", [], ["Pm16", "b6", "b7"], lambda: V.tensor_scalar(T.Pm16[:], PE, 4096.0, None, Op.add))
+        op("V", ["Pd.0", "Pd.1"], ["dP", "b6", "b7"], lambda: V.tensor_tensor(T.dP[:], PE, T.Pd[:], Op.subtract))
+
+    def mates_less_self(t):
+        op("V", ["min0" if t == 0 else "min1", "vf"], ["dT"],
+           lambda: V.tensor_tensor(T.dT[:], T["min"][:, t * K:(t + 1) * K], T.vf[:], Op.subtract))
+
+    def minus_twice(t, engs):
+        X = "X%d" % t
+        for u, e in zip((0, 2, 4, 6), engs):
+            if e == "V":
+                op("V", ks(X, u, 1), ks("Xm2", u, 1),
+                   lambda: V.tensor_scalar(un("Xm2", u), un(X, u), -2.0, None, Op.mult))
+            else:
+                op("A", ks(X, u, 1), ks("Xm2", u, 1),
+                   lambda: A.activation(un("Xm2", u), un(X, u), Fn.Identity, scale=-2.0))
+
+    sent = [0]
+
+    def write(c, src, to, sem, m):
+        a = topo.addr(c)
+        sent[0] += popcount(m)
+        return RemoteDMATransfer(dst_ids=[DstId(rid=a[0], pnc=a[1])], dma_engine_mask=m, remote_sem=T.sem[sem],
+                                 src=src, dst=to)
+
+    def send_block(t, q):
+        X, Y, s = "X%d" % t, "Y%d" % t, "arrY%d" % t
+        before("G", ks(X, 2 * q, 2), [])
+        if prv_far and q in HANDED:
+            tr = [write(hlp, un(X, 2 * q), un(Y, 2 * q), "arr%s%d" % ("YZB"[HANDED.index(q)], t), R["rest"]),
+                  write(prv, un(X, 2 * q + 1), un(Y, 2 * q + 1), s, topo.mask(core, prv))]
+        else:
+            tr = [write(prv, un(X, 2 * q, 2), un(Y, 2 * q, 2), s, topo.mask(core, prv))]
+        g.remote_dma_fused(tr, local_sem=T.sem.sent)
+
+    def send_late(t):
+        X, Z, s = T["X%d" % t], T["Z%d" % t], "arrZ%d" % t
+        if prv_far:
+            g.remote_dma_fused([write(nxt, X[:], Z[:], s, R["rest"])], local_sem=T.sem.sent)
+        else:
+            need("G", writer["Y%d" % t])
+            g.remote_dma_fused([write(hlp, X[:, 0:2 * BL], Z[:, 0:2 * BL], s, R["rest"]),
+                                write(nxt, X[:, 2 * BL:], Z[:, 2 * BL:], s, topo.mask(core, nxt))],
+                               local_sem=T.sem.sent)
+
+    for t in range(RO):
+        ny = 4 * popcount(topo.mask(nxt, core))
+        if prv_far:
+            nz = popcount(topo.mask(prv, core)) + popcount(topo.mask(RG[prv]["help"], core))
+        else:
+            ny += len(HANDED) * popcount(topo.mask(RG[nxt]["help"], core))
+            nz = popcount(RG[prv]["rest"])
+        writer["Y%d" % t] = ("arrY%d" % t, ny)
+        writer["Z%d" % t] = ("arrZ%d" % t, nz)
+        writer["Bin%d" % t] = ("arrB%d" % t, popcount(topo.mask(prv, core)))
+
+    g.sync.dma_start(T.pin[:], T.p[:]).then_inc(T.sem.ldp, 16)
+    writer["pin"] = ("ldp", 16)
+    g.scalar.dma_start(T["min"][:, 0:K], T.mate[:, 0:K]).then_inc(T.sem.ldm, 16)
+    writer["min0"] = ("ldm", 16)
+    for q in range(4):
+        g.sync.dma_start(un("X0", 2 * q, 2), T.x[:, q * BL:(q + 1) * BL]).then_inc(T.sem["ldx%d" % q], 16)
+        for k in ks("X0", 2 * q, 2):
+            writer[k] = ("ldx%d" % q, 16)
+    g.sync.dma_start(T["min"][:, K:], T.mate[:, K:]).then_inc(T.sem.ldn, 16)
+    writer["min1"] = ("ldn", 16)
+
+    kw = {"allow_small_or_imprecise_dtypes": True}
+    op("G", [], ["pi"], lambda: g.iota(T.pi[:], [[0, 1]], 0, 1))
+    op("G", [], ["qr"], lambda: g.iota(T.qr[:], [[1, 16]], 0, 0, **kw))
+    op("G", [], ["rr"], lambda: g.iota(T.rr[:], [[1, K]], 0, 0, **kw))
+    op("G", [], ["gr"], lambda: g.iota(T.gr[:], [[1, 8], [0, 16]], 0, 0, **kw))
+    op("G", [], ["dg"], lambda: g.iota(T.dg[:], [[1, 128]], 0, -1, **kw))
+    op("G", [], ["c16"], lambda: g.iota(T.c16[:], [[16, K]], 0, 0, **kw))
+    for q in range(4):
+        send_block(0, q)
+    send_late(0)
+    op("V", [], ["Zp"], lambda: V.memset(T.Zp[:], 0.0))
+    op("V", ["pi"], ["ki"], lambda: V.tensor_scalar(T.ki[:], T.pi[:], 15, None, Op.bitwise_and))
+    op("V", ["pi"], ["gi"], lambda: V.tensor_scalar(T.gi[:], T.pi[:], 4, None, Op.arith_shift_right))
+    op("V", ["ki"], ["kf"], lambda: V.tensor_copy(T.kf[:], T.ki[:]))
+    op("V", ["gi"], ["gf"], lambda: V.tensor_copy(T.gf[:], T.gi[:]))
+    op("V", ["qr", "kf"], ["A16"], lambda: V.tensor_scalar(T.A16[:], T.qr[:], T.kf[:], None, Op.is_equal))
+    op("V", ["qr", "kf"], ["C16"], lambda: V.tensor_scalar(T.C16[:], T.qr[:], T.kf[:], 256.0, Op.is_gt, Op.mult))
+    op("V", ["gr", "gf"], ["BD"], lambda: V.tensor_scalar(T.BD[:], T.gr[:], T.gf[:], None, Op.is_equal))
+    op("V", ["kf"], ["bT"], lambda: V.tensor_scalar(T.bT[:], T.kf[:], -256.0, 2048.0, Op.mult, Op.add))
+    op("V", ["BD"], ["Zp"], lambda: V.tensor_copy(T.Zp[:, 15:143:16], T.BD[:, 0:128:16]))
+    for i in range(16):
+        op("A", ["BD", "A16"], ["Xs.%d" % i],
+           lambda: A.activation(T.Xs[:, 128 * i:128 * (i + 1)], T.BD[:], Fn.Identity, scale=T.A16[:, i:i + 1]))
+    op("A", ["Zp"], ["Zn"], lambda: A.activation(T.Zn[:], T.Zp[:], Fn.Identity, scale=-1.0))
+    for q in range(16):
+        op("V", ["rr", "A16", "C16"], ["W.s%d" % q],
+           lambda: V.tensor_scalar(T.W[:, K * q:K * (q + 1)], T.rr[:], T.A16[:, q:q + 1], T.C16[:, q:q + 1],
+                                   Op.mult, Op.add))
+        if q == 9:
+            op("V", ["pin"], ["Pc"], lambda: V.tensor_scalar(T.Pc[:], T.pin[:], -2048.0, None, Op.add))
+    op("V", ["pin"], ["P16.0", "P16.1"], lambda: V.tensor_copy(T.P16[:], T.pin[:]))
+    op("V", ["min0"], ["m16"], lambda: V.tensor_copy(T.m16[:, 0:K], T["min"][:, 0:K]))
+    op("V", ["dg"], ["I1"], lambda: V.tensor_scalar(T.I1[:], T.dg[:], 0.0, None, Op.is_equal))
+    op("V", ["P16.0", "P16.1"] + ["W.s%d" % q for q in range(16)], ks("Dif") + ks("W"),
+       lambda: V.tensor_copy(T.Dif[:, 0:V_].indirect(T.P16[:]), T.W[:]))
+    table("Pc", "A" * 8, ["Pc"])
+    pick("m16", 0, "AAAA", "m16")
+    fold("Dif", 0, "Zp", True, True, 2, 4)
+    fold("Dif", 2, "Zp", True, True, 2, 4)
+    op("A", ["I1"], ["In"], lambda: A.activation(T.In[:], T.I1[:], Fn.Identity, scale=-1.0))
+    op("A", ["I1"], ["I2"], lambda: A.activation(T.I2[:], T.I1[:], Fn.Identity, scale=-2.0))
+    op("A", ["c16", "kf"], ["vf"], lambda: A.activation(T.vf[:], T.c16[:], Fn.Identity, bias=T.kf[:]))
+    op("A", ["vf"], ["vc"], lambda: A.activation(T.vc[:], T.vf[:], Fn.Identity, bias=-2048.0))
+    minus_twice(0, "AAAA")
+    op("V", ["pin"], ["Pd.0", "Pd.1"], lambda: V.tensor_scalar(T.Pd[:], T.pin[:], -4096.0, None, Op.add))
+    mates_links()
+    mates_less_self(0)
+    op("V", ["min1"], ["m16b"], lambda: V.tensor_copy(T.m16[:, K:], T["min"][:, K:]))
+    op("V", [], ["B0", "b4", "b5"], lambda: V.tensor_copy(T.B0[:], seam(4)))
+
+    outs = [0]
+    PL = ["P16.0", "P16.1"]
+    for t in range(RO):
+        X, Xn, Y, Z = "X%d" % t, "X%d" % (t + 1), "Y%d" % t, "Z%d" % t
+        yw, zw, dw, Bin = T[Y][:, 0:V_], T[Z][:, 0:V_], T.Dif[:, 0:V_], "Bin%d" % t
+        mk = "m16" if t == 0 else "m16b"
+
+        def vsum(out, win, wk, lname, other, u, n, alu):
+            op("V", [wk, lname] + PL + ks(other, u, n), ks(out, u, n),
+               lambda: V.tensor_tensor(un(out, u, n), win.indirect(lst(lname, u, n)), un(other, u, n), alu))
+
+        def aget(out, win, wk, lname, u, n):
+            op("A", [wk, lname] + PL, ks(out, u, n),
+               lambda: A.activation(un(out, u, n), win.indirect(lst(lname, u, n)), Fn.Copy))
+
+        def acopy(out, u, b, n=1, fn=Fn.Copy):
+            op("A", [], ks(out, u, n) + bk(b, n), lambda: A.activation(un(out, u, n), bank(b, n), fn))
+
+        aget("S", yw, Y, "P16", 4, 2)
+        aget("S", yw, Y, "P16", 6, 2)
+        vsum("M1", yw, Y, "P16", X, 0, 2, Op.max)
+        vsum("M2", yw, Y, "Pm16", X, 4, 2, Op.max)
+        vsum("M2", yw, Y, "Pm16", X, 6, 2, Op.max)
+        vsum("M2", yw, Y, "Pm16", X, 0, 2, Op.max)
+        vsum("M1", yw, Y, "P16", X, 2, 2, Op.max)
+        vsum("M2", yw, Y, "Pm16", X, 2, 1, Op.max)
+        vsum("M2", yw, Y, "Pm16", X, 3, 1, Op.max)
+        mm([("In", X), ("I1", "S")], 4, 0, n=2)
+        mm([("In", X), ("I1", "S")], 6, 2, n=2)
+        acopy("R1", 4, 0, 2, Fn.Relu)
+        acopy("R1", 6, 2, 2, Fn.Relu)
+        mm([("I1", X), ("In", "M2")], 4, 4, True, False, n=2)
+        mm([("I1", "R1")], 4, 4, False, True, n=2)
+        mm([("I1", X), ("In", "M2")], 6, 0, True, False, n=2)
+        mm([("I1", "R1")], 6, 0, False, True, n=2)
+        acopy("Dif", 4, 4, 2)
+        mm([("I1", "M1"), ("In", "M2")], 0, 2, n=2)
+        acopy("Dif", 6, 0, 2)
+        acopy("Dif", 0, 2, 2)
+        mm([("I1", "M1")], 2, 4, True, False, n=2)
+        mm([("In", "M2")], 2, 4, False, True, n=2)
+        fold("Dif", 2, "Zp", True, False, 2)
+        acopy("Dif", 2, 4)
+        op("V", [], ["Dif.3", "b5"], lambda: V.tensor_copy(un("Dif", 3), bank(5)))
+        fold("Dif", 0, "Zp", True, False, 2)
+        for q in range(4):
+            w, o = dw.indirect(lst("m16", 2 * q, 2, t * K)), un("GD", 2 * q, 2)
+            if q % 2 == 0:
+                op("V", ks("Dif") + [mk], ks("GD", 2 * q, 2), lambda: V.tensor_copy(o, w))
+            else:
+                op("A", ks("Dif") + [mk], ks("GD", 2 * q, 2), lambda: A.activation(o, w, Fn.Copy))
+            fold("GD", q, "Zp", False, q % 2 == 1)
+        Bn = "B%d" % (t + 1)
+
+        def half(name, h):
+            return T[name][:, h * H:(h + 1) * H]
+
+        def new_links(h, go, qq):
+            op("V", ["dP"], ["b4", "b5"], lambda: V.tensor_tensor(qq, go, half("dP", h), Op.mult))
+            op("V", [], ["Pd.%d" % h, "b4"], lambda: V.tensor_tensor(half("Pd", h), qq, half("Pd", h), Op.add))
+            op("V", ["Pd.%d" % h], [PL[h]], lambda: V.tensor_scalar(half("P16", h), half("Pd", h), 4096.0, None, Op.add))
+
+        for h in (0, 1):
+            go, qq = ps[:, 5 * U + h * H:5 * U + (h + 1) * H], ps[:, 4 * U + h * H:4 * U + (h + 1) * H]
+            e = ps[:, 7 * U + (h - 1) * H:7 * U + h * H]
+            op("V", [], ["b5", "b%d" % (6 + h)], lambda: V.tensor_scalar(go, e, 0.0, None, Op.is_gt))
+            op("V", ["dT"], ["b4", "b5"], lambda: V.tensor_tensor(qq, go, half("dT", h), Op.mult))
+            op("V", ["vc"], ["Tc.%d" % h, "b4"], lambda: V.tensor_tensor(half("Tc", h), qq, half("vc", h), Op.add))
+            new_links(h, go, qq)
+        table("Tc", "AVAVAVAA", ["Tc.0", "Tc.1"])
+        pick("B%d" % t, 0, "VAVA", "B%d" % t)
+        vsum("W1", yw, Y, "P16", "Xm2", 0, 1, Op.add)
+        op("V", [], [Bn, "b6", "b7"], lambda: V.tensor_scalar(T[Bn][:], PE, 4096.0, None, Op.add))
+        before("G", [Bn], [])
+        g.remote_dma_fused([write(nxt, T[Bn][:], T[Bin][:], "arrB%d" % t, topo.mask(core, nxt))],
+                           local_sem=T.sem.sent)
+        for u in (1, 3, 5, 7):
+            aget("W1", yw, Y, "P16", u, 1)
+        for u in (2, 4, 6):
+            vsum("W1", yw, Y, "P16", "Xm2", u, 1, Op.add)
+        if t == RO - 1:
+            op("A", ["Pd.0", "Pd.1"], ["ypf"], lambda: A.activation(T.ypf[:], T.Pd[:], Fn.Identity, bias=4096.0))
+            before("S", ["ypf"], [])
+            g.sync.dma_start(T.yp[:], T.ypf[:]).then_inc(T.sem.out, 16)
+            outs[0] += 16
+        else:
+            op("V", ["Pd.0", "Pd.1"], ["Pc"], lambda: V.tensor_scalar(T.Pc[:], T.Pd[:], 2048.0, None, Op.add))
+
+        def vpred(u):
+            vsum("W", zw, Z, Bin, "W1", u, 1, Op.add)
+            op("V", ks("W", u, 1), ks("Cl", u, 1),
+               lambda: V.tensor_scalar(un("Cl", u), un("W", u), CL, -CL, Op.min, Op.max))
+
+        def apred(u):
+            aget("W", zw, Z, Bin, u, 1)
+            mm([("I1", "W")], u, u // 2, False, True)
+
+        def vclip(u):
+            op("V", [], ks("Cl", u, 1) + bk(u // 2),
+               lambda: V.tensor_scalar(un("Cl", u), bank(u // 2), CL, -CL, Op.min, Op.max))
+
+        def step(u):
+            mm([("I1", "Cl")], u, 4 + u % 4, False, True)
+
+        def new(u):
+            acopy(Xn, u, 4 + u % 4)
+            if u < 4:
+                mm([("I1", X)], u + 4, 4 + u, True, u == 3)
+
+        def done(q):
+            if t < RO - 1:
+                send_block(t + 1, q)
+            else:
+                before("S", ks(Xn, 2 * q, 2), [])
+                g.sync.dma_start(T.yx[:, q * BL:(q + 1) * BL], un(Xn, 2 * q, 2)).then_inc(T.sem.out, 16)
+                outs[0] += 16
+
+        mm([("I1", X)], 0, 4, True, False, n=4)
+        for u in (1, 3, 5, 7):
+            mm([("I2", X), ("I1", "W1")], u, u // 2, True, False)
+        apred(1)
+        vpred(0)
+        step(0)
+        apred(3)
+        vclip(1)
+        step(1)
+        new(0)
+        vpred(2)
+        step(2)
+        new(1)
+        done(0)
+        vclip(3)
+        step(3)
+        apred(5)
+        new(2)
+        vpred(4)
+        step(4)
+        new(3)
+        done(1)
+        vclip(5)
+        step(5)
+        apred(7)
+        new(4)
+        vpred(6)
+        step(6)
+        new(5)
+        done(2)
+        vclip(7)
+        op("V", ["Cl.7"], [Xn + ".7", "b7"], lambda: V.tensor_tensor(un(Xn, 7), bank(7), un("Cl", 7), Op.add))
+        new(6)
+        done(3)
+        if t < RO - 1:
+            send_late(t + 1)
+            table("Pc", "AVAVAVAV", ["Pc"])
+            pick("m16", (t + 1) * K, "VAVA", "m16b")
+            mates_less_self(t + 1)
+            minus_twice(t + 1, "VVAA")
+            mates_links()
+
+    for e in "VATG":
+        need("G", ("s" + e, cnt[e]))
+    g.wait_ge(T.sem.sent, sent[0])
+    g.wait_ge(T.sem.out, outs[0])

@@ -7,6 +7,7 @@ BL = 2 * U
 K = V_ // 16
 H = K // 2
 HANDED = (0, 1, 2)
+SA, SV = (1, 3), (0,)
 
 SCRATCH = {"ps": ("psum", [128, 4096], "float32")}
 for _t in range(RO + 1):
@@ -18,24 +19,27 @@ for _t in range(RO):
     SCRATCH["Bin%d" % _t] = ("sbuf", [128, K], "uint16")
 for _n in ("M1", "M2", "S", "R1", "Dif", "GD", "tab", "W1", "W", "Cl", "Xm2"):
     SCRATCH[_n] = ("sbuf", [128, V_], "bfloat16")
+for _n in ("Ph", "Pl", "Th", "Tl", "rr"):
+    SCRATCH[_n] = ("sbuf", [128, K], "bfloat16")
+for _n in ("Pd", "dP", "dT", "vf", "c16"):
+    SCRATCH[_n] = ("sbuf", [128, K], "float32")
+for _n in ("P16", "Pm16", "Bp", "mp"):
+    SCRATCH[_n] = ("sbuf", [128, K], "uint16")
+for _n in ("pin", "Bi", "mi", "ci"):
+    SCRATCH[_n] = ("sbuf", [128, K], "int32")
 SCRATCH.update({
-    "pin": ("sbuf", [128, K], "int32"), "min": ("sbuf", [128, RO * K], "int32"),
-    "m16": ("sbuf", [128, RO * K], "uint16"), "P16": ("sbuf", [128, K], "uint16"), "Pm16": ("sbuf", [128, K], "uint16"),
-    "Pd": ("sbuf", [128, K], "float32"), "dP": ("sbuf", [128, K], "float32"), "dT": ("sbuf", [128, K], "float32"),
-    "Pc": ("sbuf", [128, K], "float16"), "Tc": ("sbuf", [128, K], "float16"), "ypf": ("sbuf", [128, K], "float32"),
-    "vf": ("sbuf", [128, K], "float32"), "vc": ("sbuf", [128, K], "float32"), "c16": ("sbuf", [128, K], "float32"),
-    "rr": ("sbuf", [128, K], "bfloat16"),
+    "min": ("sbuf", [128, RO * K], "int32"), "m16": ("sbuf", [128, RO * K], "uint16"),
     "pi": ("sbuf", [128, 1], "int32"), "ki": ("sbuf", [128, 1], "int32"), "gi": ("sbuf", [128, 1], "int32"),
-    "kf": ("sbuf", [128, 1], "float32"), "gf": ("sbuf", [128, 1], "float32"), "bT": ("sbuf", [128, 1], "float32"),
+    "kf": ("sbuf", [128, 1], "float32"), "gf": ("sbuf", [128, 1], "float32"), "k2": ("sbuf", [128, 1], "float32"),
     "qr": ("sbuf", [128, 16], "float32"), "A16": ("sbuf", [128, 16], "float32"), "C16": ("sbuf", [128, 16], "float32"),
     "gr": ("sbuf", [128, 128], "float32"), "dg": ("sbuf", [128, 128], "float32"),
     "BD": ("sbuf", [128, 128], "bfloat16"), "I1": ("sbuf", [128, 128], "bfloat16"),
     "In": ("sbuf", [128, 128], "bfloat16"), "I2": ("sbuf", [128, 128], "bfloat16"),
-    "Zp": ("sbuf", [128, 144], "bfloat16"), "Zn": ("sbuf", [128, 144], "bfloat16"),
-    "Xs": ("sbuf", [128, 2048], "bfloat16"),
+    "Zp": ("sbuf", [128, 144], "bfloat16"), "Zt": ("sbuf", [128, 144], "bfloat16"),
 })
 SEMAPHORES = (["sV", "sA", "sT", "sG", "ldp", "ldm", "ldn", "sent", "out"] + ["ldx%d" % q for q in range(4)]
-              + ["arr%s%d" % (n, t) for n in "YZB" for t in range(RO)])
+              + ["arr%s%d" % (n, t) for n in "YZBC" for t in range(RO)]
+              + ["tab%s%d" % (n, t) for n in "TP" for t in range(RO)])
 
 
 def popcount(m):
@@ -135,6 +139,9 @@ def rank_program(g, core, T, topo):
     def lst(name, u, n, o=0):
         return T[name][:, o + 32 * u:o + 32 * (u + n)]
 
+    def half(name, h):
+        return T[name][:, h * H:(h + 1) * H]
+
     def bank(b, n=1):
         return ps[:, b * U:(b + n) * U]
 
@@ -144,8 +151,8 @@ def rank_program(g, core, T, topo):
     def seam(b):
         return ps[:, (b + 1) * U - H:(b + 1) * U + H]
 
-    TAB = ks("tab")
     PE = seam(6)
+    PL, PD = ["P16.0", "P16.1"], ["Pd.0", "Pd.1"]
     V, A, PE_ = g.vector, g.scalar, g.tensor
 
     def mm(terms, u, b, start=True, stop=True, n=1):
@@ -167,51 +174,60 @@ def rank_program(g, core, T, topo):
             return ins
         op("T", [z] + ks(name, 2 * q, 2 * n), bk(b + q // 2), f)
 
-    def table(src, engs, keys):
-        for j in range(8):
-            b = j % 4
+    def table(name, keys, hi, lo, rk, sem):
+        before("S", rk, keys)
+        g.sync.dma_start(T[name][0:128:16, :], T[hi][:]).then_inc(T.sem[sem], 16)
+        g.sync.dma_start(T[name][1:128:16, :], T[lo][:]).then_inc(T.sem[sem], 16)
+        c = dict(clock["S"])
+        c[sem] = 32
+        snap[(sem, 32)] = c
+        for k in keys:
+            writer[k] = (sem, 32)
+            readers[k] = []
+        for k in rk:
+            readers.setdefault(k, []).append((sem, 32))
 
-            def f():
-                for h in (0, 1):
-                    i = j + 8 * h
-                    ins = PE_.matmul(ps[:, b * U + h:(b + 1) * U:2], T.Xs[:, 128 * i:128 * (i + 1)], T[src][:],
-                                     True, True)
-                return ins
-            op("T", keys + ["Xs.%d" % j, "Xs.%d" % (j + 8)], bk(b), f)
-            o = T.tab[:, j::8]
-            if engs[j] == "V":
-                op("V", ["bT"], [TAB[j]] + bk(b), lambda: V.tensor_scalar(o, bank(b), T.bT[:], 0.0, Op.add, Op.max))
-            else:
-                op("A", ["bT"], [TAB[j]] + bk(b), lambda: A.activation(o, bank(b), Fn.Relu, bias=T.bT[:]))
-
-    def pick(lname, o, engs, lk):
+    def pick(name, keys, lname, engs):
         for q in range(4):
-            w = T.tab[:, 0:V_].indirect(lst(lname, 2 * q, 2, o))
-            out = un("GD", 2 * q, 2)
+            w, out = T[name][:, 0:V_].indirect(lst(lname, 2 * q, 2)), un("GD", 2 * q, 2)
             if engs[q] == "V":
-                op("V", TAB + [lk], ks("GD", 2 * q, 2),
-                   lambda: V.tensor_scalar(out, w, 256.0, 256.0, Op.min, Op.subtract))
+                op("V", keys + [lname], ks("GD", 2 * q, 2), lambda: V.tensor_copy(out, w))
             else:
-                op("A", TAB + [lk], ks("GD", 2 * q, 2), lambda: A.activation(out, w, Fn.Relu, bias=256.0, scale=-1.0))
-            fold("GD", q, "Zp" if engs[q] == "V" else "Zn", True, True)
+                op("A", keys + [lname], ks("GD", 2 * q, 2), lambda: A.activation(out, w, Fn.Copy))
+            fold("GD", q, "Zt", True, True)
+
+    def spread(out, src, r, w):
+        op("V", r, [out] + w, lambda: V.tensor_scalar(T[out][:], src, 4097.0, None, Op.mult))
+
+    def places(out, src):
+        op("V", [src], ["ci"],
+           lambda: V.tensor_scalar(T.ci[:], T[src][:], 4, V_ - 1, Op.arith_shift_right, Op.bitwise_and))
+        op("V", ["ci"], [out], lambda: V.tensor_copy(T[out][:], T.ci[:]))
+
+    def links_table(t):
+        op("A", PD, ["Ph"], lambda: A.activation(T.Ph[:], T.Pd[:], Fn.Copy))
+        op("V", PD + ["Ph"], ["Pl"], lambda: V.tensor_tensor(T.Pl[:], T.Pd[:], T.Ph[:], Op.subtract))
+        table("tab", ["tab"], "Ph", "Pl", ["Ph", "Pl"], "tabP%d" % t)
 
     def mates_links():
-        op("V", [], ["Pm16", "b6", "b7"], lambda: V.tensor_scalar(T.Pm16[:], PE, 4096.0, None, Op.add))
-        op("V", ["Pd.0", "Pd.1"], ["dP", "b6", "b7"], lambda: V.tensor_tensor(T.dP[:], PE, T.Pd[:], Op.subtract))
+        op("V", [], ["Pm16", "b6", "b7"], lambda: V.tensor_copy(T.Pm16[:], PE))
+        op("V", PD, ["dP", "b6", "b7"], lambda: V.tensor_tensor(T.dP[:], PE, T.Pd[:], Op.subtract))
+
+    def mate_in(t):
+        return T["min"][:, t * K:(t + 1) * K], "min0" if t == 0 else "min1"
 
     def mates_less_self(t):
-        op("V", ["min0" if t == 0 else "min1", "vf"], ["dT"],
-           lambda: V.tensor_tensor(T.dT[:], T["min"][:, t * K:(t + 1) * K], T.vf[:], Op.subtract))
+        src, k = mate_in(t)
+        op("V", [k, "vf"], ["dT"], lambda: V.tensor_tensor(T.dT[:], src, T.vf[:], Op.subtract))
 
-    def minus_twice(t, engs):
-        X = "X%d" % t
-        for u, e in zip((0, 2, 4, 6), engs):
-            if e == "V":
-                op("V", ks(X, u, 1), ks("Xm2", u, 1),
-                   lambda: V.tensor_scalar(un("Xm2", u), un(X, u), -2.0, None, Op.mult))
-            else:
-                op("A", ks(X, u, 1), ks("Xm2", u, 1),
-                   lambda: A.activation(un("Xm2", u), un(X, u), Fn.Identity, scale=-2.0))
+    def mates_list(t):
+        src, k = mate_in(t)
+        op("V", [k], ["m16.%d" % t], lambda: V.tensor_copy(T.m16[:, t * K:(t + 1) * K], src))
+
+    def mates_places(t):
+        src, k = mate_in(t)
+        spread("mi", src, [k], [])
+        places("mp", "mi")
 
     sent = [0]
 
@@ -250,7 +266,8 @@ def rank_program(g, core, T, topo):
             nz = popcount(RG[prv]["rest"])
         writer["Y%d" % t] = ("arrY%d" % t, ny)
         writer["Z%d" % t] = ("arrZ%d" % t, nz)
-        writer["Bin%d" % t] = ("arrB%d" % t, popcount(topo.mask(prv, core)))
+        writer["Bin%d.0" % t] = ("arrB%d" % t, popcount(topo.mask(prv, core)))
+        writer["Bin%d.1" % t] = ("arrC%d" % t, popcount(topo.mask(prv, core)))
 
     g.sync.dma_start(T.pin[:], T.p[:]).then_inc(T.sem.ldp, 16)
     writer["pin"] = ("ldp", 16)
@@ -280,52 +297,50 @@ def rank_program(g, core, T, topo):
     op("V", ["gi"], ["gf"], lambda: V.tensor_copy(T.gf[:], T.gi[:]))
     op("V", ["qr", "kf"], ["A16"], lambda: V.tensor_scalar(T.A16[:], T.qr[:], T.kf[:], None, Op.is_equal))
     op("V", ["qr", "kf"], ["C16"], lambda: V.tensor_scalar(T.C16[:], T.qr[:], T.kf[:], 256.0, Op.is_gt, Op.mult))
+    op("V", [], ["tab"], lambda: V.memset(T.tab[:], 0.0))
     op("V", ["gr", "gf"], ["BD"], lambda: V.tensor_scalar(T.BD[:], T.gr[:], T.gf[:], None, Op.is_equal))
-    op("V", ["kf"], ["bT"], lambda: V.tensor_scalar(T.bT[:], T.kf[:], -256.0, 2048.0, Op.mult, Op.add))
-    op("V", ["BD"], ["Zp"], lambda: V.tensor_copy(T.Zp[:, 15:143:16], T.BD[:, 0:128:16]))
-    for i in range(16):
-        op("A", ["BD", "A16"], ["Xs.%d" % i],
-           lambda: A.activation(T.Xs[:, 128 * i:128 * (i + 1)], T.BD[:], Fn.Identity, scale=T.A16[:, i:i + 1]))
-    op("A", ["Zp"], ["Zn"], lambda: A.activation(T.Zn[:], T.Zp[:], Fn.Identity, scale=-1.0))
-    for q in range(16):
-        op("V", ["rr", "A16", "C16"], ["W.s%d" % q],
-           lambda: V.tensor_scalar(T.W[:, K * q:K * (q + 1)], T.rr[:], T.A16[:, q:q + 1], T.C16[:, q:q + 1],
-                                   Op.mult, Op.add))
-        if q == 9:
-            op("V", ["pin"], ["Pc"], lambda: V.tensor_scalar(T.Pc[:], T.pin[:], -2048.0, None, Op.add))
-    op("V", ["pin"], ["P16.0", "P16.1"], lambda: V.tensor_copy(T.P16[:], T.pin[:]))
-    op("V", ["min0"], ["m16"], lambda: V.tensor_copy(T.m16[:, 0:K], T["min"][:, 0:K]))
+    op("V", ["kf"], ["k2"], lambda: V.tensor_scalar(T.k2[:], T.kf[:], 2.0, None, Op.is_lt))
     op("V", ["dg"], ["I1"], lambda: V.tensor_scalar(T.I1[:], T.dg[:], 0.0, None, Op.is_equal))
-    op("V", ["P16.0", "P16.1"] + ["W.s%d" % q for q in range(16)], ks("Dif") + ks("W"),
-       lambda: V.tensor_copy(T.Dif[:, 0:V_].indirect(T.P16[:]), T.W[:]))
-    table("Pc", "A" * 8, ["Pc"])
-    pick("m16", 0, "AAAA", "m16")
-    fold("Dif", 0, "Zp", True, True, 2, 4)
-    fold("Dif", 2, "Zp", True, True, 2, 4)
+    op("V", ["BD"], ["Zp"], lambda: V.tensor_copy(T.Zp[:, 15:143:16], T.BD[:, 0:128:16]))
+    NUM = ["W.s%d" % q for q in range(16)]
+
+    def numbers(q, e):
+        o, sa, sb = T.W[:, K * q:K * (q + 1)], T.A16[:, q:q + 1], T.C16[:, q:q + 1]
+        if e == "A":
+            op("A", ["rr", "A16", "C16"], [NUM[q]], lambda: A.activation(o, T.rr[:], Fn.Identity, bias=sb, scale=sa))
+        else:
+            op("V", ["rr", "A16", "C16"], [NUM[q]], lambda: V.tensor_scalar(o, T.rr[:], sa, sb, Op.mult, Op.add))
+    for q in range(9):
+        numbers(q, "A")
+    op("V", ["pin"], PD, lambda: V.tensor_copy(T.Pd[:], T.pin[:]))
+    op("V", ["pin"], PL, lambda: V.tensor_copy(T.P16[:], T.pin[:]))
+    numbers(15, "V")
+    links_table(0)
+    for q in range(9, 15):
+        numbers(q, "A")
+    mates_places(0)
+    op("V", PL + NUM, ks("Dif") + ks("W"), lambda: V.tensor_copy(T.Dif[:, 0:V_].indirect(T.P16[:]), T.W[:]))
+    op("A", ["Zp", "k2"], ["Zt"], lambda: A.activation(T.Zt[:], T.Zp[:], Fn.Identity, scale=T.k2[:]))
     op("A", ["I1"], ["In"], lambda: A.activation(T.In[:], T.I1[:], Fn.Identity, scale=-1.0))
     op("A", ["I1"], ["I2"], lambda: A.activation(T.I2[:], T.I1[:], Fn.Identity, scale=-2.0))
     op("A", ["c16", "kf"], ["vf"], lambda: A.activation(T.vf[:], T.c16[:], Fn.Identity, bias=T.kf[:]))
-    op("A", ["vf"], ["vc"], lambda: A.activation(T.vc[:], T.vf[:], Fn.Identity, bias=-2048.0))
-    minus_twice(0, "AAAA")
-    op("V", ["pin"], ["Pd.0", "Pd.1"], lambda: V.tensor_scalar(T.Pd[:], T.pin[:], -4096.0, None, Op.add))
+    pick("tab", ["tab"], "mp", "AAAA")
+    fold("Dif", 0, "Zp", True, True, 2, 4)
+    fold("Dif", 2, "Zp", True, True, 2, 4)
     mates_links()
-    mates_less_self(0)
-    op("V", ["min1"], ["m16b"], lambda: V.tensor_copy(T.m16[:, K:], T["min"][:, K:]))
-    op("V", [], ["B0", "b4", "b5"], lambda: V.tensor_copy(T.B0[:], seam(4)))
+    mates_list(0)
 
     outs = [0]
-    PL = ["P16.0", "P16.1"]
     for t in range(RO):
         X, Xn, Y, Z = "X%d" % t, "X%d" % (t + 1), "Y%d" % t, "Z%d" % t
-        yw, zw, dw, Bin = T[Y][:, 0:V_], T[Z][:, 0:V_], T.Dif[:, 0:V_], "Bin%d" % t
-        mk = "m16" if t == 0 else "m16b"
+        yw, zw, dw, Bin, Bn = T[Y][:, 0:V_], T[Z][:, 0:V_], T.Dif[:, 0:V_], "Bin%d" % t, "B%d" % (t + 1)
 
         def vsum(out, win, wk, lname, other, u, n, alu):
-            op("V", [wk, lname] + PL + ks(other, u, n), ks(out, u, n),
+            op("V", [wk, lname, "%s.%d" % (lname, u // 4)] + PL + ks(other, u, n), ks(out, u, n),
                lambda: V.tensor_tensor(un(out, u, n), win.indirect(lst(lname, u, n)), un(other, u, n), alu))
 
         def aget(out, win, wk, lname, u, n):
-            op("A", [wk, lname] + PL, ks(out, u, n),
+            op("A", [wk, lname, "%s.%d" % (lname, u // 4)] + PL, ks(out, u, n),
                lambda: A.activation(un(out, u, n), win.indirect(lst(lname, u, n)), Fn.Copy))
 
         def acopy(out, u, b, n=1, fn=Fn.Copy):
@@ -334,6 +349,8 @@ def rank_program(g, core, T, topo):
         aget("S", yw, Y, "P16", 4, 2)
         aget("S", yw, Y, "P16", 6, 2)
         vsum("M1", yw, Y, "P16", X, 0, 2, Op.max)
+        if t == 0:
+            spread("Bi", seam(4), [], ["b4", "b5"])
         vsum("M2", yw, Y, "Pm16", X, 4, 2, Op.max)
         vsum("M2", yw, Y, "Pm16", X, 6, 2, Op.max)
         vsum("M2", yw, Y, "Pm16", X, 0, 2, Op.max)
@@ -356,50 +373,62 @@ def rank_program(g, core, T, topo):
         mm([("In", "M2")], 2, 4, False, True, n=2)
         fold("Dif", 2, "Zp", True, False, 2)
         acopy("Dif", 2, 4)
-        op("V", [], ["Dif.3", "b5"], lambda: V.tensor_copy(un("Dif", 3), bank(5)))
+        acopy("Dif", 3, 5)
+        mates_less_self(t)
         fold("Dif", 0, "Zp", True, False, 2)
         for q in range(4):
             w, o = dw.indirect(lst("m16", 2 * q, 2, t * K)), un("GD", 2 * q, 2)
             if q % 2 == 0:
-                op("V", ks("Dif") + [mk], ks("GD", 2 * q, 2), lambda: V.tensor_copy(o, w))
+                op("V", ks("Dif") + ["m16.%d" % t], ks("GD", 2 * q, 2), lambda: V.tensor_copy(o, w))
             else:
-                op("A", ks("Dif") + [mk], ks("GD", 2 * q, 2), lambda: A.activation(o, w, Fn.Copy))
+                op("A", ks("Dif") + ["m16.%d" % t], ks("GD", 2 * q, 2), lambda: A.activation(o, w, Fn.Copy))
             fold("GD", q, "Zp", False, q % 2 == 1)
-        Bn = "B%d" % (t + 1)
-
-        def half(name, h):
-            return T[name][:, h * H:(h + 1) * H]
-
-        def new_links(h, go, qq):
-            op("V", ["dP"], ["b4", "b5"], lambda: V.tensor_tensor(qq, go, half("dP", h), Op.mult))
-            op("V", [], ["Pd.%d" % h, "b4"], lambda: V.tensor_tensor(half("Pd", h), qq, half("Pd", h), Op.add))
-            op("V", ["Pd.%d" % h], [PL[h]], lambda: V.tensor_scalar(half("P16", h), half("Pd", h), 4096.0, None, Op.add))
+        for u in (0, 2, 4, 6):
+            op("A", ks(X, u, 1), ks("Xm2", u, 1), lambda: A.activation(un("Xm2", u), un(X, u), Fn.Identity, scale=-2.0))
 
         for h in (0, 1):
             go, qq = ps[:, 5 * U + h * H:5 * U + (h + 1) * H], ps[:, 4 * U + h * H:4 * U + (h + 1) * H]
             e = ps[:, 7 * U + (h - 1) * H:7 * U + h * H]
             op("V", [], ["b5", "b%d" % (6 + h)], lambda: V.tensor_scalar(go, e, 0.0, None, Op.is_gt))
             op("V", ["dT"], ["b4", "b5"], lambda: V.tensor_tensor(qq, go, half("dT", h), Op.mult))
-            op("V", ["vc"], ["Tc.%d" % h, "b4"], lambda: V.tensor_tensor(half("Tc", h), qq, half("vc", h), Op.add))
-            new_links(h, go, qq)
-        table("Tc", "AVAVAVAA", ["Tc.0", "Tc.1"])
-        pick("B%d" % t, 0, "VAVA", "B%d" % t)
-        vsum("W1", yw, Y, "P16", "Xm2", 0, 1, Op.add)
-        op("V", [], [Bn, "b6", "b7"], lambda: V.tensor_scalar(T[Bn][:], PE, 4096.0, None, Op.add))
-        before("G", [Bn], [])
-        g.remote_dma_fused([write(nxt, T[Bn][:], T[Bin][:], "arrB%d" % t, topo.mask(core, nxt))],
-                           local_sem=T.sem.sent)
-        for u in (1, 3, 5, 7):
+            op("V", ["vf"], ["b4"], lambda: V.tensor_tensor(qq, qq, half("vf", h), Op.add))
+            op("V", [], ["Th.%d" % h, "b4"], lambda: V.tensor_copy(half("Th", h), qq))
+            op("V", ["Th.%d" % h], ["Tl.%d" % h, "b4"],
+               lambda: V.tensor_tensor(half("Tl", h), qq, half("Th", h), Op.subtract))
+        table("M2", ks("M2"), "Th", "Tl", ["Th.0", "Th.1", "Tl.0", "Tl.1"], "tabT%d" % t)
+        go, qq = ps[:, 5 * U:5 * U + K], ps[:, 4 * U:4 * U + K]
+        op("V", ["dP"], ["b4", "b5"], lambda: V.tensor_tensor(qq, go, T.dP[:], Op.mult))
+        op("V", [], PD + ["b4"], lambda: V.tensor_tensor(T.Pd[:], qq, T.Pd[:], Op.add))
+        op("V", PD, PL, lambda: V.tensor_copy(T.P16[:], T.Pd[:]))
+        if t == 0:
+            places("Bp", "Bi")
+        for u in SA:
             aget("W1", yw, Y, "P16", u, 1)
-        for u in (2, 4, 6):
+        for u in SV:
+            vsum("W1", yw, Y, "P16", "Xm2", u, 1, Op.add)
+        pick("M2", ks("M2"), "Bp", "VAVA")
+        rest = [u for u in (0, 2, 4, 6) if u not in SV]
+        for h in (0, 1):
+            e = ps[:, 7 * U + (h - 1) * H:7 * U + h * H]
+            op("V", [], ["%s.%d" % (Bn, h), "b%d" % (6 + h)], lambda: V.tensor_copy(half(Bn, h), e))
+            before("G", ["%s.%d" % (Bn, h)], [])
+            g.remote_dma_fused([write(nxt, half(Bn, h), half(Bin, h), "arr%s%d" % ("BC"[h], t), topo.mask(core, nxt))],
+                               local_sem=T.sem.sent)
+            if h == 0:
+                vsum("W1", yw, Y, "P16", "Xm2", rest[0], 1, Op.add)
+        if t < RO - 1:
+            spread("Bi", PE, [], ["b6", "b7"])
+        for u in (1, 3, 5, 7):
+            if u not in SA:
+                aget("W1", yw, Y, "P16", u, 1)
+        for u in rest[1:]:
             vsum("W1", yw, Y, "P16", "Xm2", u, 1, Op.add)
         if t == RO - 1:
-            op("A", ["Pd.0", "Pd.1"], ["ypf"], lambda: A.activation(T.ypf[:], T.Pd[:], Fn.Identity, bias=4096.0))
-            before("S", ["ypf"], [])
-            g.sync.dma_start(T.yp[:], T.ypf[:]).then_inc(T.sem.out, 16)
+            before("S", PD, [])
+            g.sync.dma_start(T.yp[:], T.Pd[:]).then_inc(T.sem.out, 16)
             outs[0] += 16
         else:
-            op("V", ["Pd.0", "Pd.1"], ["Pc"], lambda: V.tensor_scalar(T.Pc[:], T.Pd[:], 2048.0, None, Op.add))
+            links_table(t + 1)
 
         def vpred(u):
             vsum("W", zw, Z, Bin, "W1", u, 1, Op.add)
@@ -466,10 +495,10 @@ def rank_program(g, core, T, topo):
         done(3)
         if t < RO - 1:
             send_late(t + 1)
-            table("Pc", "AVAVAVAV", ["Pc"])
-            pick("m16", (t + 1) * K, "VAVA", "m16b")
-            mates_less_self(t + 1)
-            minus_twice(t + 1, "VVAA")
+            mates_places(t + 1)
+            pick("tab", ["tab"], "mp", "VAVA")
+            places("Bp", "Bi")
+            mates_list(t + 1)
             mates_links()
 
     for e in "VATG":

from concourse.bass import DstId, RemoteDMATransfer
from concourse.mybir import AluOpType as Op, ActivationFunctionType as Fn

V_, RO, CL = 4096, 3, 20.0
U = 512
BL = 2 * U
K = V_ // 16
H = K // 2
HANDED = (0, 1, 2)
SA, SV = (1, 3), (0,)

SCRATCH = {"ps": ("psum", [128, 4096], "float32")}
for _t in range(RO + 1):
    SCRATCH["X%d" % _t] = ("sbuf", [128, V_], "bfloat16")
    SCRATCH["B%d" % _t] = ("sbuf", [128, K], "uint16")
for _t in range(RO):
    SCRATCH["Y%d" % _t] = ("sbuf", [128, V_], "bfloat16")
    SCRATCH["Z%d" % _t] = ("sbuf", [128, V_], "bfloat16")
    SCRATCH["Bin%d" % _t] = ("sbuf", [128, K], "uint16")
for _n in ("M1", "M2", "S", "R1", "Dif", "GD", "tab", "W1", "W", "Cl", "Xm2"):
    SCRATCH[_n] = ("sbuf", [128, V_], "bfloat16")
for _n in ("Ph", "Pl", "Th", "Tl", "rr"):
    SCRATCH[_n] = ("sbuf", [128, K], "bfloat16")
for _n in ("Pd", "dP", "dT", "vf", "c16"):
    SCRATCH[_n] = ("sbuf", [128, K], "float32")
for _n in ("P16", "Pm16", "Bp", "mp"):
    SCRATCH[_n] = ("sbuf", [128, K], "uint16")
for _n in ("pin", "Bi", "mi", "ci"):
    SCRATCH[_n] = ("sbuf", [128, K], "int32")
SCRATCH.update({
    "min": ("sbuf", [128, RO * K], "int32"), "m16": ("sbuf", [128, RO * K], "uint16"),
    "pi": ("sbuf", [128, 1], "int32"), "ki": ("sbuf", [128, 1], "int32"), "gi": ("sbuf", [128, 1], "int32"),
    "kf": ("sbuf", [128, 1], "float32"), "gf": ("sbuf", [128, 1], "float32"), "k2": ("sbuf", [128, 1], "float32"),
    "qr": ("sbuf", [128, 16], "float32"), "A16": ("sbuf", [128, 16], "float32"), "C16": ("sbuf", [128, 16], "float32"),
    "gr": ("sbuf", [128, 128], "float32"), "dg": ("sbuf", [128, 128], "float32"),
    "BD": ("sbuf", [128, 128], "bfloat16"), "I1": ("sbuf", [128, 128], "bfloat16"),
    "In": ("sbuf", [128, 128], "bfloat16"), "I2": ("sbuf", [128, 128], "bfloat16"),
    "Zp": ("sbuf", [128, 144], "bfloat16"), "Zt": ("sbuf", [128, 144], "bfloat16"),
})
SEMAPHORES = (["sV", "sA", "sT", "sG", "ldp", "ldm", "ldn", "sent", "out"] + ["ldx%d" % q for q in range(4)]
              + ["arr%s%d" % (n, t) for n in "YZBC" for t in range(RO)]
              + ["tab%s%d" % (n, t) for n in "TP" for t in range(RO)])


def popcount(m):
    return bin(m).count("1")


def ring(T, topo):
    n, taken, out = len(T.cores), [], {}
    for r, c in enumerate(T.cores):
        prv, nxt = T.cores[(r - 1) % n], T.cores[(r + 1) % n]
        far = prv if topo.chip(prv) != topo.chip(c) else nxt
        h = [x for x in topo.cores_of(c) if T.rank_of(x) is None and x not in taken
             and topo.die(x) != topo.die(c) and topo.may_write(x, far)][0]
        taken.append(h)
        out[c] = {"prv": prv, "nxt": nxt, "far": far, "help": h, "rest": topo.mask(c, h) & ~topo.mask(c, far)}
    return out


def helper_program(g, core, R, T, topo):
    far, got = R["far"], popcount(R["rest"])
    a, m, sent = topo.addr(far), topo.mask(core, far), 0
    for t in range(RO):
        if far == R["prv"]:
            pieces = [("arr%s%d" % (s, t), T["Y%d" % t][:, q * BL:q * BL + U], "arrY%d" % t)
                      for s, q in zip("YZB", HANDED)]
        else:
            pieces = [("arrZ%d" % t, T["Z%d" % t][:, 0:2 * BL], "arrZ%d" % t)]
        for here, ap, there in pieces:
            g.wait_ge(T.sem[here], got)
            g.remote_dma(ap, ap, T.sem[there], T.sem.sent, a[1], a[0], m)
            sent += popcount(m)
    g.wait_ge(T.sem.sent, sent)


def rank_program(g, core, T, topo):
    RG = ring(T, topo)
    if T.rank_of(core) is None:
        for c in T.cores:
            if RG[c]["help"] == core:
                helper_program(g, core, RG[c], T, topo)
        return
    R = RG[core]
    prv, nxt, hlp = R["prv"], R["nxt"], R["help"]
    prv_far = R["far"] == prv
    Q = {"V": g.vector, "A": g.scalar, "T": g.tensor, "G": g, "S": g.sync}
    ps = T.ps

    cnt = {e: 0 for e in Q}
    clock = {e: {} for e in Q}
    snap = {}
    writer, readers = {}, {}

    def need(e, ev):
        s, v = ev
        if e == "T" and s == "sT":
            return
        if clock[e].get(s, 0) >= v:
            return
        Q[e].wait_ge(T.sem[s], v)
        for a, b in snap.get(ev, {s: v}).items():
            if clock[e].get(a, 0) < b:
                clock[e][a] = b

    def before(e, r, w):
        evs = [writer[k] for k in r if k in writer]
        for k in w:
            if k in writer:
                evs.append(writer[k])
            evs += readers.get(k, [])
        best = {}
        for s, v in evs:
            best[s] = max(best.get(s, 0), v)
        for s in sorted(best):
            need(e, (s, best[s]))

    def op(e, r, w, f):
        before(e, r, w)
        ins = f()
        cnt[e] += 1
        ev = ("s" + e, cnt[e])
        ins.then_inc(T.sem["s" + e], 1)
        c = dict(clock[e])
        c[ev[0]] = ev[1]
        snap[ev] = c
        for k in r:
            readers.setdefault(k, []).append(ev)
        for k in w:
            writer[k] = ev
            readers[k] = []

    def un(name, u, n=1):
        return T[name][:, u * U:(u + n) * U]

    def ks(name, u=0, n=8):
        return ["%s.%d" % (name, x) for x in range(u, u + n)]

    def lst(name, u, n, o=0):
        return T[name][:, o + 32 * u:o + 32 * (u + n)]

    def half(name, h):
        return T[name][:, h * H:(h + 1) * H]

    def bank(b, n=1):
        return ps[:, b * U:(b + n) * U]

    def bk(b, n=1):
        return ["b%d" % x for x in range(b, b + n)]

    def seam(b):
        return ps[:, (b + 1) * U - H:(b + 1) * U + H]

    PE = seam(6)
    PL, PD = ["P16.0", "P16.1"], ["Pd.0", "Pd.1"]
    V, A, PE_ = g.vector, g.scalar, g.tensor

    def mm(terms, u, b, start=True, stop=True, n=1):
        for x in range(n):
            def f():
                for j, (mat, name) in enumerate(terms):
                    ins = PE_.matmul(bank(b + x), T[mat][:], un(name, u + x),
                                     start and j == 0, stop and j == len(terms) - 1)
                return ins
            op("T", [m for m, _ in terms] + ["%s.%d" % (nm, u + x) for _, nm in terms], bk(b + x), f)

    def fold(name, q, z, start, stop, n=1, b=6):
        e0 = (b + 1) * U - H

        def f():
            for i in range(16):
                ins = PE_.matmul(ps[:, e0 + 64 * q:e0 + 64 * (q + n)], T[z][:, 15 - i:143 - i],
                                 T[name][:, q * BL + i:(q + n) * BL:16], start and i == 0, stop and i == 15)
            return ins
        op("T", [z] + ks(name, 2 * q, 2 * n), bk(b + q // 2), f)

    def table(name, keys, hi, lo, rk, sem):
        before("S", rk, keys)
        g.sync.dma_start(T[name][0:128:16, :], T[hi][:]).then_inc(T.sem[sem], 16)
        g.sync.dma_start(T[name][1:128:16, :], T[lo][:]).then_inc(T.sem[sem], 16)
        c = dict(clock["S"])
        c[sem] = 32
        snap[(sem, 32)] = c
        for k in keys:
            writer[k] = (sem, 32)
            readers[k] = []
        for k in rk:
            readers.setdefault(k, []).append((sem, 32))

    def pick(name, keys, lname, engs):
        for q in range(4):
            w, out = T[name][:, 0:V_].indirect(lst(lname, 2 * q, 2)), un("GD", 2 * q, 2)
            if engs[q] == "V":
                op("V", keys + [lname], ks("GD", 2 * q, 2), lambda: V.tensor_copy(out, w))
            else:
                op("A", keys + [lname], ks("GD", 2 * q, 2), lambda: A.activation(out, w, Fn.Copy))
            fold("GD", q, "Zt", True, True)

    def spread(out, src, r, w):
        op("V", r, [out] + w, lambda: V.tensor_scalar(T[out][:], src, 4097.0, None, Op.mult))

    def places(out, src):
        op("V", [src], ["ci"],
           lambda: V.tensor_scalar(T.ci[:], T[src][:], 4, V_ - 1, Op.arith_shift_right, Op.bitwise_and))
        op("V", ["ci"], [out], lambda: V.tensor_copy(T[out][:], T.ci[:]))

    def links_table(t):
        op("A", PD, ["Ph"], lambda: A.activation(T.Ph[:], T.Pd[:], Fn.Copy))
        op("V", PD + ["Ph"], ["Pl"], lambda: V.tensor_tensor(T.Pl[:], T.Pd[:], T.Ph[:], Op.subtract))
        table("tab", ["tab"], "Ph", "Pl", ["Ph", "Pl"], "tabP%d" % t)

    def mates_links():
        op("V", [], ["Pm16", "b6", "b7"], lambda: V.tensor_copy(T.Pm16[:], PE))
        op("V", PD, ["dP", "b6", "b7"], lambda: V.tensor_tensor(T.dP[:], PE, T.Pd[:], Op.subtract))

    def mate_in(t):
        return T["min"][:, t * K:(t + 1) * K], "min0" if t == 0 else "min1"

    def mates_less_self(t):
        src, k = mate_in(t)
        op("V", [k, "vf"], ["dT"], lambda: V.tensor_tensor(T.dT[:], src, T.vf[:], Op.subtract))

    def mates_list(t):
        src, k = mate_in(t)
        op("V", [k], ["m16.%d" % t], lambda: V.tensor_copy(T.m16[:, t * K:(t + 1) * K], src))

    def mates_places(t):
        src, k = mate_in(t)
        spread("mi", src, [k], [])
        places("mp", "mi")

    sent = [0]

    def write(c, src, to, sem, m):
        a = topo.addr(c)
        sent[0] += popcount(m)
        return RemoteDMATransfer(dst_ids=[DstId(rid=a[0], pnc=a[1])], dma_engine_mask=m, remote_sem=T.sem[sem],
                                 src=src, dst=to)

    def send_block(t, q):
        X, Y, s = "X%d" % t, "Y%d" % t, "arrY%d" % t
        before("G", ks(X, 2 * q, 2), [])
        if prv_far and q in HANDED:
            tr = [write(hlp, un(X, 2 * q), un(Y, 2 * q), "arr%s%d" % ("YZB"[HANDED.index(q)], t), R["rest"]),
                  write(prv, un(X, 2 * q + 1), un(Y, 2 * q + 1), s, topo.mask(core, prv))]
        else:
            tr = [write(prv, un(X, 2 * q, 2), un(Y, 2 * q, 2), s, topo.mask(core, prv))]
        g.remote_dma_fused(tr, local_sem=T.sem.sent)

    def send_late(t):
        X, Z, s = T["X%d" % t], T["Z%d" % t], "arrZ%d" % t
        if prv_far:
            g.remote_dma_fused([write(nxt, X[:], Z[:], s, R["rest"])], local_sem=T.sem.sent)
        else:
            need("G", writer["Y%d" % t])
            g.remote_dma_fused([write(hlp, X[:, 0:2 * BL], Z[:, 0:2 * BL], s, R["rest"]),
                                write(nxt, X[:, 2 * BL:], Z[:, 2 * BL:], s, topo.mask(core, nxt))],
                               local_sem=T.sem.sent)

    for t in range(RO):
        ny = 4 * popcount(topo.mask(nxt, core))
        if prv_far:
            nz = popcount(topo.mask(prv, core)) + popcount(topo.mask(RG[prv]["help"], core))
        else:
            ny += len(HANDED) * popcount(topo.mask(RG[nxt]["help"], core))
            nz = popcount(RG[prv]["rest"])
        writer["Y%d" % t] = ("arrY%d" % t, ny)
        writer["Z%d" % t] = ("arrZ%d" % t, nz)
        writer["Bin%d.0" % t] = ("arrB%d" % t, popcount(topo.mask(prv, core)))
        writer["Bin%d.1" % t] = ("arrC%d" % t, popcount(topo.mask(prv, core)))

    g.sync.dma_start(T.pin[:], T.p[:]).then_inc(T.sem.ldp, 16)
    writer["pin"] = ("ldp", 16)
    g.scalar.dma_start(T["min"][:, 0:K], T.mate[:, 0:K]).then_inc(T.sem.ldm, 16)
    writer["min0"] = ("ldm", 16)
    for q in range(4):
        g.sync.dma_start(un("X0", 2 * q, 2), T.x[:, q * BL:(q + 1) * BL]).then_inc(T.sem["ldx%d" % q], 16)
        for k in ks("X0", 2 * q, 2):
            writer[k] = ("ldx%d" % q, 16)
    g.sync.dma_start(T["min"][:, K:], T.mate[:, K:]).then_inc(T.sem.ldn, 16)
    writer["min1"] = ("ldn", 16)

    kw = {"allow_small_or_imprecise_dtypes": True}
    op("G", [], ["pi"], lambda: g.iota(T.pi[:], [[0, 1]], 0, 1))
    op("G", [], ["qr"], lambda: g.iota(T.qr[:], [[1, 16]], 0, 0, **kw))
    op("G", [], ["rr"], lambda: g.iota(T.rr[:], [[1, K]], 0, 0, **kw))
    op("G", [], ["gr"], lambda: g.iota(T.gr[:], [[1, 8], [0, 16]], 0, 0, **kw))
    op("G", [], ["dg"], lambda: g.iota(T.dg[:], [[1, 128]], 0, -1, **kw))
    op("G", [], ["c16"], lambda: g.iota(T.c16[:], [[16, K]], 0, 0, **kw))
    for q in range(4):
        send_block(0, q)
    send_late(0)
    op("V", [], ["Zp"], lambda: V.memset(T.Zp[:], 0.0))
    op("V", ["pi"], ["ki"], lambda: V.tensor_scalar(T.ki[:], T.pi[:], 15, None, Op.bitwise_and))
    op("V", ["pi"], ["gi"], lambda: V.tensor_scalar(T.gi[:], T.pi[:], 4, None, Op.arith_shift_right))
    op("V", ["ki"], ["kf"], lambda: V.tensor_copy(T.kf[:], T.ki[:]))
    op("V", ["gi"], ["gf"], lambda: V.tensor_copy(T.gf[:], T.gi[:]))
    op("V", ["qr", "kf"], ["A16"], lambda: V.tensor_scalar(T.A16[:], T.qr[:], T.kf[:], None, Op.is_equal))
    op("V", ["qr", "kf"], ["C16"], lambda: V.tensor_scalar(T.C16[:], T.qr[:], T.kf[:], 256.0, Op.is_gt, Op.mult))
    op("V", [], ["tab"], lambda: V.memset(T.tab[:], 0.0))
    op("V", ["gr", "gf"], ["BD"], lambda: V.tensor_scalar(T.BD[:], T.gr[:], T.gf[:], None, Op.is_equal))
    op("V", ["kf"], ["k2"], lambda: V.tensor_scalar(T.k2[:], T.kf[:], 2.0, None, Op.is_lt))
    op("V", ["dg"], ["I1"], lambda: V.tensor_scalar(T.I1[:], T.dg[:], 0.0, None, Op.is_equal))
    op("V", ["BD"], ["Zp"], lambda: V.tensor_copy(T.Zp[:, 15:143:16], T.BD[:, 0:128:16]))
    NUM = ["W.s%d" % q for q in range(16)]

    def numbers(q, e):
        o, sa, sb = T.W[:, K * q:K * (q + 1)], T.A16[:, q:q + 1], T.C16[:, q:q + 1]
        if e == "A":
            op("A", ["rr", "A16", "C16"], [NUM[q]], lambda: A.activation(o, T.rr[:], Fn.Identity, bias=sb, scale=sa))
        else:
            op("V", ["rr", "A16", "C16"], [NUM[q]], lambda: V.tensor_scalar(o, T.rr[:], sa, sb, Op.mult, Op.add))
    for q in range(9):
        numbers(q, "A")
    op("V", ["pin"], PD, lambda: V.tensor_copy(T.Pd[:], T.pin[:]))
    op("V", ["pin"], PL, lambda: V.tensor_copy(T.P16[:], T.pin[:]))
    numbers(15, "V")
    links_table(0)
    for q in range(9, 15):
        numbers(q, "A")
    mates_places(0)
    op("V", PL + NUM, ks("Dif") + ks("W"), lambda: V.tensor_copy(T.Dif[:, 0:V_].indirect(T.P16[:]), T.W[:]))
    op("A", ["Zp", "k2"], ["Zt"], lambda: A.activation(T.Zt[:], T.Zp[:], Fn.Identity, scale=T.k2[:]))
    op("A", ["I1"], ["In"], lambda: A.activation(T.In[:], T.I1[:], Fn.Identity, scale=-1.0))
    op("A", ["I1"], ["I2"], lambda: A.activation(T.I2[:], T.I1[:], Fn.Identity, scale=-2.0))
    op("A", ["c16", "kf"], ["vf"], lambda: A.activation(T.vf[:], T.c16[:], Fn.Identity, bias=T.kf[:]))
    pick("tab", ["tab"], "mp", "AAAA")
    fold("Dif", 0, "Zp", True, True, 2, 4)
    fold("Dif", 2, "Zp", True, True, 2, 4)
    mates_links()
    mates_list(0)

    outs = [0]
    for t in range(RO):
        X, Xn, Y, Z = "X%d" % t, "X%d" % (t + 1), "Y%d" % t, "Z%d" % t
        yw, zw, dw, Bin, Bn = T[Y][:, 0:V_], T[Z][:, 0:V_], T.Dif[:, 0:V_], "Bin%d" % t, "B%d" % (t + 1)

        def vsum(out, win, wk, lname, other, u, n, alu):
            op("V", [wk, lname, "%s.%d" % (lname, u // 4)] + PL + ks(other, u, n), ks(out, u, n),
               lambda: V.tensor_tensor(un(out, u, n), win.indirect(lst(lname, u, n)), un(other, u, n), alu))

        def aget(out, win, wk, lname, u, n):
            op("A", [wk, lname, "%s.%d" % (lname, u // 4)] + PL, ks(out, u, n),
               lambda: A.activation(un(out, u, n), win.indirect(lst(lname, u, n)), Fn.Copy))

        def acopy(out, u, b, n=1, fn=Fn.Copy):
            op("A", [], ks(out, u, n) + bk(b, n), lambda: A.activation(un(out, u, n), bank(b, n), fn))

        aget("S", yw, Y, "P16", 4, 2)
        aget("S", yw, Y, "P16", 6, 2)
        vsum("M1", yw, Y, "P16", X, 0, 2, Op.max)
        if t == 0:
            spread("Bi", seam(4), [], ["b4", "b5"])
        vsum("M2", yw, Y, "Pm16", X, 4, 2, Op.max)
        vsum("M2", yw, Y, "Pm16", X, 6, 2, Op.max)
        vsum("M2", yw, Y, "Pm16", X, 0, 2, Op.max)
        vsum("M1", yw, Y, "P16", X, 2, 2, Op.max)
        vsum("M2", yw, Y, "Pm16", X, 2, 1, Op.max)
        vsum("M2", yw, Y, "Pm16", X, 3, 1, Op.max)
        mm([("In", X), ("I1", "S")], 4, 0, n=2)
        mm([("In", X), ("I1", "S")], 6, 2, n=2)
        acopy("R1", 4, 0, 2, Fn.Relu)
        acopy("R1", 6, 2, 2, Fn.Relu)
        mm([("I1", X), ("In", "M2")], 4, 4, True, False, n=2)
        mm([("I1", "R1")], 4, 4, False, True, n=2)
        mm([("I1", X), ("In", "M2")], 6, 0, True, False, n=2)
        mm([("I1", "R1")], 6, 0, False, True, n=2)
        acopy("Dif", 4, 4, 2)
        mm([("I1", "M1"), ("In", "M2")], 0, 2, n=2)
        acopy("Dif", 6, 0, 2)
        acopy("Dif", 0, 2, 2)
        mm([("I1", "M1")], 2, 4, True, False, n=2)
        mm([("In", "M2")], 2, 4, False, True, n=2)
        fold("Dif", 2, "Zp", True, False, 2)
        acopy("Dif", 2, 4)
        acopy("Dif", 3, 5)
        mates_less_self(t)
        fold("Dif", 0, "Zp", True, False, 2)
        for q in range(4):
            w, o = dw.indirect(lst("m16", 2 * q, 2, t * K)), un("GD", 2 * q, 2)
            if q % 2 == 0:
                op("V", ks("Dif") + ["m16.%d" % t], ks("GD", 2 * q, 2), lambda: V.tensor_copy(o, w))
            else:
                op("A", ks("Dif") + ["m16.%d" % t], ks("GD", 2 * q, 2), lambda: A.activation(o, w, Fn.Copy))
            fold("GD", q, "Zp", False, q % 2 == 1)
        for u in (0, 2, 4, 6):
            op("A", ks(X, u, 1), ks("Xm2", u, 1), lambda: A.activation(un("Xm2", u), un(X, u), Fn.Identity, scale=-2.0))

        for h in (0, 1):
            go, qq = ps[:, 5 * U + h * H:5 * U + (h + 1) * H], ps[:, 4 * U + h * H:4 * U + (h + 1) * H]
            e = ps[:, 7 * U + (h - 1) * H:7 * U + h * H]
            op("V", [], ["b5", "b%d" % (6 + h)], lambda: V.tensor_scalar(go, e, 0.0, None, Op.is_gt))
            op("V", ["dT"], ["b4", "b5"], lambda: V.tensor_tensor(qq, go, half("dT", h), Op.mult))
            op("V", ["vf"], ["b4"], lambda: V.tensor_tensor(qq, qq, half("vf", h), Op.add))
            op("V", [], ["Th.%d" % h, "b4"], lambda: V.tensor_copy(half("Th", h), qq))
            op("V", ["Th.%d" % h], ["Tl.%d" % h, "b4"],
               lambda: V.tensor_tensor(half("Tl", h), qq, half("Th", h), Op.subtract))
        table("M2", ks("M2"), "Th", "Tl", ["Th.0", "Th.1", "Tl.0", "Tl.1"], "tabT%d" % t)
        go, qq = ps[:, 5 * U:5 * U + K], ps[:, 4 * U:4 * U + K]
        op("V", ["dP"], ["b4", "b5"], lambda: V.tensor_tensor(qq, go, T.dP[:], Op.mult))
        op("V", [], PD + ["b4"], lambda: V.tensor_tensor(T.Pd[:], qq, T.Pd[:], Op.add))
        op("V", PD, PL, lambda: V.tensor_copy(T.P16[:], T.Pd[:]))
        if t == 0:
            places("Bp", "Bi")
        for u in SA:
            aget("W1", yw, Y, "P16", u, 1)
        for u in SV:
            vsum("W1", yw, Y, "P16", "Xm2", u, 1, Op.add)
        pick("M2", ks("M2"), "Bp", "VAVA")
        rest = [u for u in (0, 2, 4, 6) if u not in SV]
        for h in (0, 1):
            e = ps[:, 7 * U + (h - 1) * H:7 * U + h * H]
            op("V", [], ["%s.%d" % (Bn, h), "b%d" % (6 + h)], lambda: V.tensor_copy(half(Bn, h), e))
            before("G", ["%s.%d" % (Bn, h)], [])
            g.remote_dma_fused([write(nxt, half(Bn, h), half(Bin, h), "arr%s%d" % ("BC"[h], t), topo.mask(core, nxt))],
                               local_sem=T.sem.sent)
            if h == 0:
                vsum("W1", yw, Y, "P16", "Xm2", rest[0], 1, Op.add)
        if t < RO - 1:
            spread("Bi", PE, [], ["b6", "b7"])
        for u in (1, 3, 5, 7):
            if u not in SA:
                aget("W1", yw, Y, "P16", u, 1)
        for u in rest[1:]:
            vsum("W1", yw, Y, "P16", "Xm2", u, 1, Op.add)
        if t == RO - 1:
            before("S", PD, [])
            g.sync.dma_start(T.yp[:], T.Pd[:]).then_inc(T.sem.out, 16)
            outs[0] += 16
        else:
            links_table(t + 1)

        def vpred(u):
            vsum("W", zw, Z, Bin, "W1", u, 1, Op.add)
            op("V", ks("W", u, 1), ks("Cl", u, 1),
               lambda: V.tensor_scalar(un("Cl", u), un("W", u), CL, -CL, Op.min, Op.max))

        def apred(u):
            aget("W", zw, Z, Bin, u, 1)
            mm([("I1", "W")], u, u // 2, False, True)

        def vclip(u):
            op("V", [], ks("Cl", u, 1) + bk(u // 2),
               lambda: V.tensor_scalar(un("Cl", u), bank(u // 2), CL, -CL, Op.min, Op.max))

        def step(u):
            mm([("I1", "Cl")], u, 4 + u % 4, False, True)

        def new(u):
            acopy(Xn, u, 4 + u % 4)
            if u < 4:
                mm([("I1", X)], u + 4, 4 + u, True, u == 3)

        def done(q):
            if t < RO - 1:
                send_block(t + 1, q)
            else:
                before("S", ks(Xn, 2 * q, 2), [])
                g.sync.dma_start(T.yx[:, q * BL:(q + 1) * BL], un(Xn, 2 * q, 2)).then_inc(T.sem.out, 16)
                outs[0] += 16

        mm([("I1", X)], 0, 4, True, False, n=4)
        for u in (1, 3, 5, 7):
            mm([("I2", X), ("I1", "W1")], u, u // 2, True, False)
        apred(1)
        vpred(0)
        step(0)
        apred(3)
        vclip(1)
        step(1)
        new(0)
        vpred(2)
        step(2)
        new(1)
        done(0)
        vclip(3)
        step(3)
        apred(5)
        new(2)
        vpred(4)
        step(4)
        new(3)
        done(1)
        vclip(5)
        step(5)
        apred(7)
        new(4)
        vpred(6)
        step(6)
        new(5)
        done(2)
        vclip(7)
        op("V", ["Cl.7"], [Xn + ".7", "b7"], lambda: V.tensor_tensor(un(Xn, 7), bank(7), un("Cl", 7), Op.add))
        new(6)
        done(3)
        if t < RO - 1:
            send_late(t + 1)
            mates_places(t + 1)
            pick("tab", ["tab"], "mp", "VAVA")
            places("Bp", "Bi")
            mates_list(t + 1)
            mates_links()

    for e in "VATG":
        need("G", ("s" + e, cnt[e]))
    g.wait_ge(T.sem.sent, sent[0])
    g.wait_ge(T.sem.out, outs[0])
